import numpy as np
import ml_dtypes


def mxq(x, axis, fmt="e4m3"):
    dtype, down = {"e4m3": (ml_dtypes.float8_e4m3fn, 7), "e5m2": (ml_dtypes.float8_e5m2, 14)}[fmt]
    v = np.moveaxis(np.asarray(x, np.float32).astype(ml_dtypes.bfloat16).astype(np.float64), axis, -1)
    blocks = v.reshape(v.shape[:-1] + (-1, 32))
    amax = np.abs(blocks).max(-1, keepdims=True)
    byte = np.maximum(np.where(amax > 0, np.frexp(amax)[1] - 1 + 127, 0) - down, 1)
    scale = np.exp2(byte - 127.0)
    codes = (blocks / scale).astype(np.float32).astype(dtype).astype(np.float64)
    return np.moveaxis((codes * scale).reshape(v.shape), -1, axis)


WIDE = False


def mx_kscale(k):
    if not WIDE:
        return np.ones(k)
    levels = np.array([10, -10, 5, -5, 0])
    if k % 512:
        return np.exp2(np.random.permutation(np.resize(levels, k // 32))).repeat(32)
    a = np.empty((k // 512, 16))
    for p in range(k // 512):
        a[p, :8] = np.random.permutation(np.resize(levels, 8))
        for g in range(8):
            far = levels[np.abs(levels - a[p, g]) >= 10]
            a[p, g + 8] = far[np.random.randint(len(far))]
    return np.exp2(a.ravel()).repeat(32)


def f64(x):
    return np.asarray(x).astype(np.float64)


def striped(idx):
    return np.tile(np.asarray(idx).reshape(-1, 16).T, (8, 1)).astype(np.uint16)


def unstriped(offs):
    return offs[:16].T.reshape(-1).astype(np.int64)


E2M1 = np.array([0.0, 0.5, 1.0, 1.5, 2.0, 3.0, 4.0, 6.0, -0.0, -0.5, -1.0, -1.5, -2.0, -3.0, -4.0, -6.0])


def pack_weight(w, fmt):
    k, n = w.shape
    w = f64(np.asarray(w, np.float32).astype(ml_dtypes.bfloat16)).reshape(k // 32, 32, n)
    amax = np.abs(w).max(1)
    if fmt == "e4m3":
        byte = np.frexp(amax)[1] - 1 + 127 - 7
    else:
        mant, ex = np.frexp(amax / 6.0)
        byte = np.where(mant > 0.5, ex, ex - 1) + 127
    byte = np.clip(np.where(amax > 0, byte, 1), 1, 254)
    scaled = (w * np.exp2(127.0 - byte)[:, None, :]).reshape(k, n).astype(np.float32)
    by_word = np.ascontiguousarray(scaled.reshape(k // 512, 128, 4, n).transpose(0, 1, 3, 2))
    if fmt == "e4m3":
        words = by_word.astype(ml_dtypes.float8_e4m3fn).view(np.uint8)
    else:
        c = by_word.astype(ml_dtypes.float4_e2m1fn).view(np.uint8) & 0xF
        words = (c[..., 0::2] | (c[..., 1::2] << 4)).reshape(k // 512, 128, 2 * n)
    return np.ascontiguousarray(words), np.ascontiguousarray(byte.astype(np.uint8).reshape(k // 512, 16, n))


def unpack_weight(words, scales, fmt):
    g, _, n = scales.shape
    words = np.ascontiguousarray(words).reshape(g, 128, n, -1)
    if fmt == "e4m3":
        vals = words.view(ml_dtypes.float8_e4m3fn).astype(np.float64)
    else:
        nib = np.empty((g, 128, n, 4), np.uint8)
        nib[..., 0::2] = words & 0xF
        nib[..., 1::2] = words >> 4
        vals = E2M1[nib]
    vals = vals * np.repeat(np.exp2(scales.astype(np.float64) - 127.0), 8, axis=1)[..., None]
    return vals.transpose(0, 1, 3, 2).reshape(g * 512, n)


B, N, T, D, NQ = 1, 512, 2048, 512, 256


def setup_inputs():
    n = np.random.standard_normal
    idx = np.random.permutation(T)[:B * N]
    s = mx_kscale(D)[:, None]
    kp = pack_weight(n((D, T)) / s, "e4m3")
    return {
        "qT": (n((B, D, NQ)) * s * (1.00 / np.sqrt(D))).astype(np.float32),
        "k_words": kp[0],
        "k_scales": kp[1],
        "ps": np.tile(np.random.randint(0, 64, 2048), (128, 1)).astype(np.float32),
        "sl": (np.random.uniform(0.01, 0.1, (B, NQ, 1))).astype(np.float32),
        "pq": (np.random.randint(0, 64, (B, NQ, 1))).astype(np.float32),
        "offs": striped(idx),
    }


def reference(qT, k_words, k_scales, ps, sl, pq, offs):
    idx = unstriped(offs)
    pick = lambda x, which: x[:, which].reshape(x.shape[0], B, -1).transpose(1, 0, 2)
    k = unpack_weight(k_words, k_scales, "e4m3")
    kg = pick(k, idx)
    qq = mxq(f64(qT), 1, "e4m3")
    a = qq.transpose(0, 2, 1) @ kg
    y = a - f64(sl) * np.abs(pick(f64(ps), idx)[:, :1, :] - f64(pq))
    return y

@@ -1,0 +1,123 @@
+from contextlib import ExitStack
+
+import concourse.mybir as mybir
+from concourse.masks import make_identity
+
+N, T, D, NQ = 512, 2048, 512, 256
+FLOPS = 2 * NQ * N * D
+BYTES = 4 * D * NQ + D * T + 16 * T + 4 * T + 8 * NQ + 2 * 128 * (N // 16) + 4 * NQ * N
+
+F32 = mybir.dt.float32
+BF16 = mybir.dt.bfloat16
+I32 = mybir.dt.int32
+U32 = mybir.dt.uint32
+U16 = mybir.dt.uint16
+U8 = mybir.dt.uint8
+FP8X4 = mybir.dt.float8_e4m3fn_x4
+ACT = mybir.ActivationFunctionType
+ALU = mybir.AluOpType
+
+P = 128
+PACK = 4
+QT = NQ // P
+HALVES = 2
+HALF = N // HALVES
+BLOCKS = HALF // P
+PS_ROW = 8
+
+
+def tile_attend_alibi_topk_kernel(tc, qT, k_words, k_scales, ps, sl, pq, offs, out):
+    nc = tc.nc
+    with ExitStack() as ctx:
+        keep = ctx.enter_context(tc.tile_pool(name="keep", bufs=1))
+        psum = ctx.enter_context(tc.psum_pool(name="psum", bufs=1))
+
+        offsets = keep.tile([P, N // 16], U16, name="offsets")
+        nc.sync.dma_start(offsets[:], offs)
+
+        pq_col = keep.tile([P, QT], F32, name="pq_col")
+        sl_col = keep.tile([P, QT], F32, name="sl_col")
+        nc.scalar.dma_start(sl_col[:], sl[0].rearrange("(p c) o -> p (c o)", c=QT))
+        nc.scalar.dma_start(pq_col[:], pq[0].rearrange("(p c) o -> p (c o)", c=QT))
+        neg_sl = keep.tile([P, QT], F32, name="neg_sl")
+        nc.scalar.activation(neg_sl[:], sl_col[:], ACT.Copy, scale=-1.0)
+
+        scale_pool = keep.tile([P, T // 4], I32, name="scale_pool", align_bytes=64)
+        ps_pool = keep.tile([P, T], F32, name="ps_pool", tag="ps_pool", align_bytes=64)
+        nc.vector.memset(scale_pool[:], 0)
+        nc.vector.memset(ps_pool[:], 0.0)
+
+        q_raw = keep.tile([P, PACK, NQ], F32, name="q_raw")
+        nc.sync.dma_start(q_raw[:], qT[0].rearrange("(p t) n -> p t n", t=PACK))
+        word_pool = keep.tile([P, T], I32, name="word_pool", align_bytes=64)
+        nc.sync.dma_start(word_pool[:], k_words[0].rearrange("p n t -> p (n t)").bitcast(I32))
+
+        scale_rows = k_scales[0].bitcast(I32)
+        for quad in range(4):
+            nc.scalar.dma_start(scale_pool[32 * quad : 32 * quad + 4, :], scale_rows[4 * quad : 4 * quad + 4, :])
+        nc.scalar.dma_start(ps_pool[PS_ROW : PS_ROW + 1, :], ps[0:1, :])
+
+        ident = keep.tile([P, P], F32, name="ident")
+        make_identity(nc, ident[:])
+
+        key_scales = keep.tile([P, N], U8, name="key_scales", align_bytes=64)
+        nc.vector.tensor_copy(key_scales[:], scale_pool[:].bitcast(U8).indirect(offsets[:]))
+
+        q_bf = keep.tile([P, QT, P, PACK], BF16, name="q_bf", align_bytes=64)
+        q_view = q_raw[:].rearrange("p t (m c) -> p c m t", c=QT)
+        for c in range(QT):
+            nc.scalar.copy(q_bf[:, c, :, :], q_view[:, c, :, :])
+
+        dist = []
+        for h in range(HALVES):
+            listed = offsets[:, h * HALF // 16 : (h + 1) * HALF // 16]
+            ps_row = keep.tile([P, HALF], F32, name=f"ps_row{h}", tag=f"ps_row{h}", align_bytes=64)
+            nc.vector.tensor_copy(ps_row[:], ps_pool[:].indirect(listed))
+            turned = psum.tile([P, BLOCKS, P], F32, name=f"turned{h}")
+            for b in range(BLOCKS):
+                nc.tensor.transpose(turned[:, b, :], ps_row[:, b * P : (b + 1) * P], ident[:])
+            ps_col = keep.tile([P, BLOCKS], F32, name=f"ps_col{h}")
+            nc.scalar.copy(ps_col[:], turned[:, :, PS_ROW])
+            spread = psum.tile([P, HALF], F32, name=f"spread{h}")
+            for b in range(BLOCKS):
+                nc.tensor.transpose(
+                    spread[:, b * P : (b + 1) * P], ps_col[:, b : b + 1].to_broadcast([P, P]), ident[:]
+                )
+            dist_h = keep.tile([P, QT, HALF], F32, name=f"dist{h}")
+            for c in range(QT):
+                nc.scalar.activation(dist_h[:, c, :], spread[:], ACT.Abs, bias=pq_col[:, c : c + 1], scale=-1.0)
+            dist.append(dist_h)
+
+        q_codes = keep.tile([P, NQ], U32, name="q_codes", tag="ps_row0", align_bytes=64)
+        q_scales = keep.tile([P, NQ], U8, name="q_scales", align_bytes=64)
+        nc.vector.quantize_mx(
+            out=q_codes[:].bitcast(FP8X4),
+            scales=q_scales[:],
+            in_=q_bf[:].rearrange("p c m t -> p (c m t)"),
+        )
+
+        keys = keep.tile([P, N], U32, name="keys", tag="ps_pool", align_bytes=64)
+        for h in range(HALVES):
+            listed = offsets[:, h * HALF // 16 : (h + 1) * HALF // 16]
+            nc.vector.tensor_copy(keys[:, h * HALF : (h + 1) * HALF], word_pool[:].bitcast(U32).indirect(listed))
+
+        out_rows = out[0].rearrange("(p c) n -> p c n", c=QT)
+        for h in range(HALVES):
+            slots = slice(h * HALF, (h + 1) * HALF)
+            scores = psum.tile([P, QT, HALF], F32, name=f"scores{h}")
+            for c in range(QT):
+                nc.tensor.matmul_mx(
+                    out=scores[:, c, :],
+                    lhsT=q_codes[:, c * P : (c + 1) * P].bitcast(FP8X4),
+                    lhsT_scale=q_scales[:, c * P : (c + 1) * P],
+                    rhs=keys[:, slots].bitcast(FP8X4),
+                    rhs_scale=key_scales[:, slots],
+                    start=True,
+                    stop=True,
+                )
+            for c in range(QT):
+                result = keep.tile([P, HALF], F32, name=f"result{h}_{c}")
+                nc.vector.scalar_tensor_tensor(
+                    result[:], dist[h][:, c, :], neg_sl[:, c : c + 1], scores[:, c, :], ALU.mult, ALU.add
+                )
+                nc.sync.dma_start(out_rows[:, c, slots], result[:])

@@ -36,32 +36,31 @@ def tile_attend_alibi_topk_kernel(tc, qT, k_words, k_scales, ps, sl, pq, offs, o
         nc.sync.dma_start(offsets[:], offs)
 
         pq_col = keep.tile([P, QT], F32, name="pq_col")
-        sl_col = keep.tile([P, QT], F32, name="sl_col")
+        sl_col = keep.tile([P, QT], F32, name="sl_col", tag="word_pool", align_bytes=64)
         nc.scalar.dma_start(sl_col[:], sl[0].rearrange("(p c) o -> p (c o)", c=QT))
         nc.scalar.dma_start(pq_col[:], pq[0].rearrange("(p c) o -> p (c o)", c=QT))
-        neg_sl = keep.tile([P, QT], F32, name="neg_sl")
-        nc.scalar.activation(neg_sl[:], sl_col[:], ACT.Copy, scale=-1.0)
+        neg_pq = keep.tile([P, QT], F32, name="neg_pq")
+        nc.scalar.activation(neg_pq[:], pq_col[:], ACT.Copy, scale=-1.0)
 
         scale_pool = keep.tile([P, T // 4], I32, name="scale_pool", align_bytes=64)
-        ps_pool = keep.tile([P, T], F32, name="ps_pool", tag="ps_pool", align_bytes=64)
-        nc.vector.memset(scale_pool[:], 0)
+        ps_pool = keep.tile([P, T], F32, name="ps_pool", align_bytes=64)
         nc.vector.memset(ps_pool[:], 0.0)
+        nc.vector.memset(scale_pool[:], 0)
 
         q_raw = keep.tile([P, PACK, NQ], F32, name="q_raw")
         nc.sync.dma_start(q_raw[:], qT[0].rearrange("(p t) n -> p t n", t=PACK))
-        word_pool = keep.tile([P, T], I32, name="word_pool", align_bytes=64)
-        nc.sync.dma_start(word_pool[:], k_words[0].rearrange("p n t -> p (n t)").bitcast(I32))
 
+        nc.sync.dma_start(ps_pool[PS_ROW : PS_ROW + 1, :], ps[0:1, :])
         scale_rows = k_scales[0].bitcast(I32)
         for quad in range(4):
-            nc.scalar.dma_start(scale_pool[32 * quad : 32 * quad + 4, :], scale_rows[4 * quad : 4 * quad + 4, :])
-        nc.scalar.dma_start(ps_pool[PS_ROW : PS_ROW + 1, :], ps[0:1, :])
+            nc.sync.dma_start(scale_pool[32 * quad : 32 * quad + 4, :], scale_rows[4 * quad : 4 * quad + 4, :])
 
+        neg_sl = keep.tile([P, QT], F32, name="neg_sl")
+        nc.vector.tensor_scalar(neg_sl[:], sl_col[:], -1.0, None, ALU.mult)
+        word_pool = keep.tile([P, T], I32, name="word_pool", tag="word_pool", align_bytes=64)
+        nc.sync.dma_start(word_pool[:], k_words[0].rearrange("p n t -> p (n t)").bitcast(I32))
         ident = keep.tile([P, P], F32, name="ident")
         make_identity(nc, ident[:])
-
-        key_scales = keep.tile([P, N], U8, name="key_scales", align_bytes=64)
-        nc.vector.tensor_copy(key_scales[:], scale_pool[:].bitcast(U8).indirect(offsets[:]))
 
         q_bf = keep.tile([P, QT, P, PACK], BF16, name="q_bf", align_bytes=64)
         q_view = q_raw[:].rearrange("p t (m c) -> p c m t", c=QT)
@@ -85,8 +84,11 @@ def tile_attend_alibi_topk_kernel(tc, qT, k_words, k_scales, ps, sl, pq, offs, o
                 )
             dist_h = keep.tile([P, QT, HALF], F32, name=f"dist{h}")
             for c in range(QT):
-                nc.scalar.activation(dist_h[:, c, :], spread[:], ACT.Abs, bias=pq_col[:, c : c + 1], scale=-1.0)
+                nc.scalar.activation(dist_h[:, c, :], spread[:], ACT.Abs, bias=neg_pq[:, c : c + 1])
             dist.append(dist_h)
+
+        key_scales = keep.tile([P, N], U8, name="key_scales", align_bytes=64)
+        nc.vector.tensor_copy(key_scales[:], scale_pool[:].bitcast(U8).indirect(offsets[:]))
 
         q_codes = keep.tile([P, NQ], U32, name="q_codes", tag="ps_row0", align_bytes=64)
         q_scales = keep.tile([P, NQ], U8, name="q_scales", align_bytes=64)
@@ -96,7 +98,7 @@ def tile_attend_alibi_topk_kernel(tc, qT, k_words, k_scales, ps, sl, pq, offs, o
             in_=q_bf[:].rearrange("p c m t -> p (c m t)"),
         )
 
-        keys = keep.tile([P, N], U32, name="keys", tag="ps_pool", align_bytes=64)
+        keys = keep.tile([P, N], U32, name="keys", align_bytes=64)
         for h in range(HALVES):
             listed = offsets[:, h * HALF // 16 : (h + 1) * HALF // 16]
             nc.vector.tensor_copy(keys[:, h * HALF : (h + 1) * HALF], word_pool[:].bitcast(U32).indirect(listed))
@@ -104,10 +106,10 @@ def tile_attend_alibi_topk_kernel(tc, qT, k_words, k_scales, ps, sl, pq, offs, o
         out_rows = out[0].rearrange("(p c) n -> p c n", c=QT)
         for h in range(HALVES):
             slots = slice(h * HALF, (h + 1) * HALF)
-            scores = psum.tile([P, QT, HALF], F32, name=f"scores{h}")
             for c in range(QT):
+                scores = psum.tile([P, HALF], F32, name=f"scores{h}_{c}")
                 nc.tensor.matmul_mx(
-                    out=scores[:, c, :],
+                    out=scores[:],
                     lhsT=q_codes[:, c * P : (c + 1) * P].bitcast(FP8X4),
                     lhsT_scale=q_scales[:, c * P : (c + 1) * P],
                     rhs=keys[:, slots].bitcast(FP8X4),
@@ -115,9 +117,8 @@ def tile_attend_alibi_topk_kernel(tc, qT, k_words, k_scales, ps, sl, pq, offs, o
                     start=True,
                     stop=True,
                 )
-            for c in range(QT):
                 result = keep.tile([P, HALF], F32, name=f"result{h}_{c}")
                 nc.vector.scalar_tensor_tensor(
-                    result[:], dist[h][:, c, :], neg_sl[:, c : c + 1], scores[:, c, :], ALU.mult, ALU.add
+                    result[:], dist[h][:, c, :], neg_sl[:, c : c + 1], scores[:], ALU.mult, ALU.add
                 )
                 nc.sync.dma_start(out_rows[:, c, slots], result[:])

@@ -23,7 +23,7 @@ QT = NQ // P
 HALVES = 2
 HALF = N // HALVES
 BLOCKS = HALF // P
-PS_ROW = 8
+PS_ROW = P - 1
 
 
 def tile_attend_alibi_topk_kernel(tc, qT, k_words, k_scales, ps, sl, pq, offs, out):
@@ -35,30 +35,29 @@ def tile_attend_alibi_topk_kernel(tc, qT, k_words, k_scales, ps, sl, pq, offs, o
         offsets = keep.tile([P, N // 16], U16, name="offsets")
         nc.sync.dma_start(offsets[:], offs)
 
-        pq_col = keep.tile([P, QT], F32, name="pq_col")
-        sl_col = keep.tile([P, QT], F32, name="sl_col", tag="word_pool", align_bytes=64)
-        nc.scalar.dma_start(sl_col[:], sl[0].rearrange("(p c) o -> p (c o)", c=QT))
-        nc.scalar.dma_start(pq_col[:], pq[0].rearrange("(p c) o -> p (c o)", c=QT))
-        neg_pq = keep.tile([P, QT], F32, name="neg_pq")
-        nc.scalar.activation(neg_pq[:], pq_col[:], ACT.Copy, scale=-1.0)
-
-        scale_pool = keep.tile([P, T // 4], I32, name="scale_pool", align_bytes=64)
+        scale_pool = keep.tile([P, T // 4], I32, name="scale_pool", tag="scale_pool", align_bytes=64)
         ps_pool = keep.tile([P, T], F32, name="ps_pool", align_bytes=64)
-        nc.vector.memset(ps_pool[:], 0.0)
         nc.vector.memset(scale_pool[:], 0)
+        nc.vector.memset(ps_pool[0:PS_ROW, :], 0.0)
+        nc.scalar.dma_start(ps_pool[PS_ROW : PS_ROW + 1, :], ps[0:1, :])
 
         q_raw = keep.tile([P, PACK, NQ], F32, name="q_raw")
         nc.sync.dma_start(q_raw[:], qT[0].rearrange("(p t) n -> p t n", t=PACK))
 
-        nc.sync.dma_start(ps_pool[PS_ROW : PS_ROW + 1, :], ps[0:1, :])
         scale_rows = k_scales[0].bitcast(I32)
         for quad in range(4):
             nc.sync.dma_start(scale_pool[32 * quad : 32 * quad + 4, :], scale_rows[4 * quad : 4 * quad + 4, :])
 
-        neg_sl = keep.tile([P, QT], F32, name="neg_sl")
-        nc.vector.tensor_scalar(neg_sl[:], sl_col[:], -1.0, None, ALU.mult)
-        word_pool = keep.tile([P, T], I32, name="word_pool", tag="word_pool", align_bytes=64)
+        word_pool = keep.tile([P, T], I32, name="word_pool", align_bytes=64)
         nc.sync.dma_start(word_pool[:], k_words[0].rearrange("p n t -> p (n t)").bitcast(I32))
+
+        pq_col = keep.tile([P, QT], F32, name="pq_col")
+        sl_col = keep.tile([P, QT], F32, name="sl_col")
+        nc.sync.dma_start(sl_col[:], sl[0].rearrange("(p c) o -> p (c o)", c=QT))
+        nc.sync.dma_start(pq_col[:], pq[0].rearrange("(p c) o -> p (c o)", c=QT))
+        neg_sl = keep.tile([P, QT], F32, name="neg_sl")
+        nc.scalar.activation(neg_sl[:], sl_col[:], ACT.Copy, scale=-1.0)
+
         ident = keep.tile([P, P], F32, name="ident")
         make_identity(nc, ident[:])
 
@@ -67,10 +66,11 @@ def tile_attend_alibi_topk_kernel(tc, qT, k_words, k_scales, ps, sl, pq, offs, o
         for c in range(QT):
             nc.scalar.copy(q_bf[:, c, :, :], q_view[:, c, :, :])
 
-        dist = []
+        dist = keep.tile([P, QT, N], F32, name="dist")
         for h in range(HALVES):
+            slots = slice(h * HALF, (h + 1) * HALF)
             listed = offsets[:, h * HALF // 16 : (h + 1) * HALF // 16]
-            ps_row = keep.tile([P, HALF], F32, name=f"ps_row{h}", tag=f"ps_row{h}", align_bytes=64)
+            ps_row = keep.tile([P, HALF], F32, name=f"ps_row{h}", align_bytes=64)
             nc.vector.tensor_copy(ps_row[:], ps_pool[:].indirect(listed))
             turned = psum.tile([P, BLOCKS, P], F32, name=f"turned{h}")
             for b in range(BLOCKS):
@@ -82,15 +82,13 @@ def tile_attend_alibi_topk_kernel(tc, qT, k_words, k_scales, ps, sl, pq, offs, o
                 nc.tensor.transpose(
                     spread[:, b * P : (b + 1) * P], ps_col[:, b : b + 1].to_broadcast([P, P]), ident[:]
                 )
-            dist_h = keep.tile([P, QT, HALF], F32, name=f"dist{h}")
             for c in range(QT):
-                nc.scalar.activation(dist_h[:, c, :], spread[:], ACT.Abs, bias=neg_pq[:, c : c + 1])
-            dist.append(dist_h)
+                nc.scalar.activation(dist[:, c, slots], spread[:], ACT.Abs, scale=-1.0, bias=pq_col[:, c : c + 1])
 
         key_scales = keep.tile([P, N], U8, name="key_scales", align_bytes=64)
         nc.vector.tensor_copy(key_scales[:], scale_pool[:].bitcast(U8).indirect(offsets[:]))
 
-        q_codes = keep.tile([P, NQ], U32, name="q_codes", tag="ps_row0", align_bytes=64)
+        q_codes = keep.tile([P, NQ], U32, name="q_codes", tag="scale_pool", align_bytes=64)
         q_scales = keep.tile([P, NQ], U8, name="q_scales", align_bytes=64)
         nc.vector.quantize_mx(
             out=q_codes[:].bitcast(FP8X4),
@@ -119,6 +117,6 @@ def tile_attend_alibi_topk_kernel(tc, qT, k_words, k_scales, ps, sl, pq, offs, o
                 )
                 result = keep.tile([P, HALF], F32, name=f"result{h}_{c}")
                 nc.vector.scalar_tensor_tensor(
-                    result[:], dist[h][:, c, :], neg_sl[:, c : c + 1], scores[:], ALU.mult, ALU.add
+                    result[:], dist[:, c, slots], neg_sl[:, c : c + 1], scores[:], ALU.mult, ALU.add
                 )
                 nc.sync.dma_start(out_rows[:, c, slots], result[:])

@@ -1,7 +1,6 @@
 from contextlib import ExitStack
 
 import concourse.mybir as mybir
-from concourse.masks import make_identity
 
 N, T, D, NQ = 512, 2048, 512, 256
 FLOPS = 2 * NQ * N * D
@@ -30,15 +29,29 @@ def tile_attend_alibi_topk_kernel(tc, qT, k_words, k_scales, ps, sl, pq, offs, o
     nc = tc.nc
     with ExitStack() as ctx:
         keep = ctx.enter_context(tc.tile_pool(name="keep", bufs=1))
+        late = ctx.enter_context(tc.tile_pool(name="late", bufs=1))
         psum = ctx.enter_context(tc.psum_pool(name="psum", bufs=1))
 
         offsets = keep.tile([P, N // 16], U16, name="offsets")
         nc.sync.dma_start(offsets[:], offs)
 
         scale_pool = keep.tile([P, T // 4], I32, name="scale_pool", tag="scale_pool", align_bytes=64)
-        ps_pool = keep.tile([P, T], F32, name="ps_pool", align_bytes=64)
+        ps_pool = keep.tile([P, T], F32, name="ps_pool", tag="ps_pool", align_bytes=64)
         nc.vector.memset(scale_pool[:], 0)
-        nc.vector.memset(ps_pool[0:PS_ROW, :], 0.0)
+        zeros = late.tile([P, P], F32, name="zeros", offset=0, align_bytes=64)
+        nc.vector.memset(zeros[:], 0.0)
+        ident = keep.tile([P, P], F32, name="ident")
+        nc.gpsimd.affine_select(
+            out=ident[:],
+            in_=zeros[:],
+            compare_op=ALU.not_equal,
+            fill=1.0,
+            base=0,
+            pattern=[[-1, P]],
+            channel_multiplier=1,
+        )
+        for h in range(HALVES):
+            nc.vector.memset(ps_pool[0:PS_ROW, h * T // 2 : (h + 1) * T // 2], 0.0)
         nc.scalar.dma_start(ps_pool[PS_ROW : PS_ROW + 1, :], ps[0:1, :])
 
         q_raw = keep.tile([P, PACK, NQ], F32, name="q_raw")
@@ -48,20 +61,17 @@ def tile_attend_alibi_topk_kernel(tc, qT, k_words, k_scales, ps, sl, pq, offs, o
         for quad in range(4):
             nc.sync.dma_start(scale_pool[32 * quad : 32 * quad + 4, :], scale_rows[4 * quad : 4 * quad + 4, :])
 
-        word_pool = keep.tile([P, T], I32, name="word_pool", align_bytes=64)
+        word_pool = late.tile([P, T], I32, name="word_pool", offset=128, align_bytes=64)
         nc.sync.dma_start(word_pool[:], k_words[0].rearrange("p n t -> p (n t)").bitcast(I32))
 
-        pq_col = keep.tile([P, QT], F32, name="pq_col")
-        sl_col = keep.tile([P, QT], F32, name="sl_col")
+        pq_col = late.tile([P, QT], F32, name="pq_col", offset=0, align_bytes=64)
+        sl_col = late.tile([P, QT], F32, name="sl_col", offset=64, align_bytes=64)
         nc.sync.dma_start(sl_col[:], sl[0].rearrange("(p c) o -> p (c o)", c=QT))
         nc.sync.dma_start(pq_col[:], pq[0].rearrange("(p c) o -> p (c o)", c=QT))
         neg_sl = keep.tile([P, QT], F32, name="neg_sl")
         nc.scalar.activation(neg_sl[:], sl_col[:], ACT.Copy, scale=-1.0)
 
-        ident = keep.tile([P, P], F32, name="ident")
-        make_identity(nc, ident[:])
-
-        q_bf = keep.tile([P, QT, P, PACK], BF16, name="q_bf", align_bytes=64)
+        q_bf = keep.tile([P, QT, P, PACK], BF16, name="q_bf", tag="q_bf", align_bytes=64)
         q_view = q_raw[:].rearrange("p t (m c) -> p c m t", c=QT)
         for c in range(QT):
             nc.scalar.copy(q_bf[:, c, :, :], q_view[:, c, :, :])
@@ -85,7 +95,7 @@ def tile_attend_alibi_topk_kernel(tc, qT, k_words, k_scales, ps, sl, pq, offs, o
             for c in range(QT):
                 nc.scalar.activation(dist[:, c, slots], spread[:], ACT.Abs, scale=-1.0, bias=pq_col[:, c : c + 1])
 
-        key_scales = keep.tile([P, N], U8, name="key_scales", align_bytes=64)
+        key_scales = keep.tile([P, N], U8, name="key_scales", tag="ps_pool", align_bytes=64)
         nc.vector.tensor_copy(key_scales[:], scale_pool[:].bitcast(U8).indirect(offsets[:]))
 
         q_codes = keep.tile([P, NQ], U32, name="q_codes", tag="scale_pool", align_bytes=64)
@@ -96,7 +106,7 @@ def tile_attend_alibi_topk_kernel(tc, qT, k_words, k_scales, ps, sl, pq, offs, o
             in_=q_bf[:].rearrange("p c m t -> p (c m t)"),
         )
 
-        keys = keep.tile([P, N], U32, name="keys", align_bytes=64)
+        keys = keep.tile([P, N], U32, name="keys", tag="q_bf", align_bytes=64)
         for h in range(HALVES):
             listed = offsets[:, h * HALF // 16 : (h + 1) * HALF // 16]
             nc.vector.tensor_copy(keys[:, h * HALF : (h + 1) * HALF], word_pool[:].bitcast(U32).indirect(listed))

@@ -35,11 +35,11 @@ def tile_attend_alibi_topk_kernel(tc, qT, k_words, k_scales, ps, sl, pq, offs, o
         offsets = keep.tile([P, N // 16], U16, name="offsets")
         nc.sync.dma_start(offsets[:], offs)
 
-        scale_pool = keep.tile([P, T // 4], I32, name="scale_pool", tag="scale_pool", align_bytes=64)
-        ps_pool = keep.tile([P, T], F32, name="ps_pool", tag="ps_pool", align_bytes=64)
-        nc.vector.memset(scale_pool[:], 0)
+        scale_pool = keep.tile([P, T // 4], I32, name="scale_pool", align_bytes=64)
+        ps_pool = keep.tile([P, T], F32, name="ps_pool", align_bytes=64)
         zeros = late.tile([P, P], F32, name="zeros", offset=0, align_bytes=64)
         nc.vector.memset(zeros[:], 0.0)
+        nc.vector.memset(scale_pool[:], 0)
         ident = keep.tile([P, P], F32, name="ident")
         nc.gpsimd.affine_select(
             out=ident[:],
@@ -71,7 +71,7 @@ def tile_attend_alibi_topk_kernel(tc, qT, k_words, k_scales, ps, sl, pq, offs, o
         neg_sl = keep.tile([P, QT], F32, name="neg_sl")
         nc.scalar.activation(neg_sl[:], sl_col[:], ACT.Copy, scale=-1.0)
 
-        q_bf = keep.tile([P, QT, P, PACK], BF16, name="q_bf", tag="q_bf", align_bytes=64)
+        q_bf = keep.tile([P, QT, P, PACK], BF16, name="q_bf", align_bytes=64)
         q_view = q_raw[:].rearrange("p t (m c) -> p c m t", c=QT)
         for c in range(QT):
             nc.scalar.copy(q_bf[:, c, :, :], q_view[:, c, :, :])
@@ -95,10 +95,10 @@ def tile_attend_alibi_topk_kernel(tc, qT, k_words, k_scales, ps, sl, pq, offs, o
             for c in range(QT):
                 nc.scalar.activation(dist[:, c, slots], spread[:], ACT.Abs, scale=-1.0, bias=pq_col[:, c : c + 1])
 
-        key_scales = keep.tile([P, N], U8, name="key_scales", tag="ps_pool", align_bytes=64)
+        key_scales = keep.tile([P, N], U8, name="key_scales", align_bytes=64)
         nc.vector.tensor_copy(key_scales[:], scale_pool[:].bitcast(U8).indirect(offsets[:]))
 
-        q_codes = keep.tile([P, NQ], U32, name="q_codes", tag="scale_pool", align_bytes=64)
+        q_codes = keep.tile([P, NQ], U32, name="q_codes", align_bytes=64)
         q_scales = keep.tile([P, NQ], U8, name="q_scales", align_bytes=64)
         nc.vector.quantize_mx(
             out=q_codes[:].bitcast(FP8X4),
@@ -106,10 +106,13 @@ def tile_attend_alibi_topk_kernel(tc, qT, k_words, k_scales, ps, sl, pq, offs, o
             in_=q_bf[:].rearrange("p c m t -> p (c m t)"),
         )
 
-        keys = keep.tile([P, N], U32, name="keys", tag="q_bf", align_bytes=64)
+        keys = [
+            keep.tile([P, HALF], U32, name="keys0", align_bytes=64),
+            keep.tile([P, HALF], U32, name="keys1", align_bytes=64),
+        ]
         for h in range(HALVES):
             listed = offsets[:, h * HALF // 16 : (h + 1) * HALF // 16]
-            nc.vector.tensor_copy(keys[:, h * HALF : (h + 1) * HALF], word_pool[:].bitcast(U32).indirect(listed))
+            nc.vector.tensor_copy(keys[h][:], word_pool[:].bitcast(U32).indirect(listed))
 
         out_rows = out[0].rearrange("(p c) n -> p c n", c=QT)
         for h in range(HALVES):
@@ -120,7 +123,7 @@ def tile_attend_alibi_topk_kernel(tc, qT, k_words, k_scales, ps, sl, pq, offs, o
                     out=scores[:],
                     lhsT=q_codes[:, c * P : (c + 1) * P].bitcast(FP8X4),
                     lhsT_scale=q_scales[:, c * P : (c + 1) * P],
-                    rhs=keys[:, slots].bitcast(FP8X4),
+                    rhs=keys[h][:].bitcast(FP8X4),
                     rhs_scale=key_scales[:, slots],
                     start=True,
                     stop=True,

@@ -50,8 +50,8 @@ def tile_attend_alibi_topk_kernel(tc, qT, k_words, k_scales, ps, sl, pq, offs, o
             pattern=[[-1, P]],
             channel_multiplier=1,
         )
-        for h in range(HALVES):
-            nc.vector.memset(ps_pool[0:PS_ROW, h * T // 2 : (h + 1) * T // 2], 0.0)
+        for first, last in ((0, 255), (255, 512), (512, T)):
+            nc.vector.memset(ps_pool[0:PS_ROW, first:last], 0.0)
         nc.scalar.dma_start(ps_pool[PS_ROW : PS_ROW + 1, :], ps[0:1, :])
 
         q_raw = keep.tile([P, PACK, NQ], F32, name="q_raw")

@@ -37,9 +37,9 @@ def tile_attend_alibi_topk_kernel(tc, qT, k_words, k_scales, ps, sl, pq, offs, o
 
         scale_pool = keep.tile([P, T // 4], I32, name="scale_pool", align_bytes=64)
         ps_pool = keep.tile([P, T], F32, name="ps_pool", align_bytes=64)
-        zeros = late.tile([P, P], F32, name="zeros", offset=0, align_bytes=64)
-        nc.vector.memset(zeros[:], 0.0)
+        zeros = late.tile([P, P], F32, name="zeros", offset=3008, align_bytes=64)
         nc.vector.memset(scale_pool[:], 0)
+        nc.vector.memset(zeros[:], 0.0)
         ident = keep.tile([P, P], F32, name="ident")
         nc.gpsimd.affine_select(
             out=ident[:],
@@ -54,35 +54,53 @@ def tile_attend_alibi_topk_kernel(tc, qT, k_words, k_scales, ps, sl, pq, offs, o
             nc.vector.memset(ps_pool[0:PS_ROW, first:last], 0.0)
         nc.scalar.dma_start(ps_pool[PS_ROW : PS_ROW + 1, :], ps[0:1, :])
 
-        q_raw = keep.tile([P, PACK, NQ], F32, name="q_raw")
-        nc.sync.dma_start(q_raw[:], qT[0].rearrange("(p t) n -> p t n", t=PACK))
+        q_rows = qT[0].rearrange("(p t) n -> p t n", t=PACK)
+        q_raw = [
+            keep.tile([P, PACK, P], F32, name="q_raw0"),
+            late.tile([P, PACK, P], F32, name="q_raw1", offset=1024, align_bytes=64),
+        ]
+        nc.sync.dma_start(q_raw[0][:], q_rows[:, :, 0:P])
 
         scale_rows = k_scales[0].bitcast(I32)
         for quad in range(4):
             nc.sync.dma_start(scale_pool[32 * quad : 32 * quad + 4, :], scale_rows[4 * quad : 4 * quad + 4, :])
 
-        word_pool = late.tile([P, T], I32, name="word_pool", offset=128, align_bytes=64)
+        word_pool = late.tile([P, T], I32, name="word_pool", offset=3264, align_bytes=64)
         nc.sync.dma_start(word_pool[:], k_words[0].rearrange("p n t -> p (n t)").bitcast(I32))
 
-        pq_col = late.tile([P, QT], F32, name="pq_col", offset=0, align_bytes=64)
-        sl_col = late.tile([P, QT], F32, name="sl_col", offset=64, align_bytes=64)
-        nc.sync.dma_start(sl_col[:], sl[0].rearrange("(p c) o -> p (c o)", c=QT))
-        nc.sync.dma_start(pq_col[:], pq[0].rearrange("(p c) o -> p (c o)", c=QT))
+        pq_col = late.tile([P, QT, 8], F32, name="pq_col", offset=3136, align_bytes=64)
+        sl_col = late.tile([P, QT, 8], F32, name="sl_col", offset=3200, align_bytes=64)
+        with nc.allow_non_contiguous_dma(reason="one value a partition for each query tile"):
+            nc.sync.dma_start(pq_col[:, :, 0:1], pq[0].rearrange("(c p) o -> p c o", c=QT))
+            nc.sync.dma_start(q_raw[1][:], q_rows[:, :, P : 2 * P])
+            nc.sync.dma_start(sl_col[:, :, 0:1], sl[0].rearrange("(c p) o -> p c o", c=QT))
         neg_sl = keep.tile([P, QT], F32, name="neg_sl")
-        nc.scalar.activation(neg_sl[:], sl_col[:], ACT.Copy, scale=-1.0)
+        nc.scalar.activation(neg_sl[:], sl_col[:, :, 0], ACT.Copy, scale=-1.0)
 
-        q_bf = keep.tile([P, QT, P, PACK], BF16, name="q_bf", align_bytes=64)
-        q_view = q_raw[:].rearrange("p t (m c) -> p c m t", c=QT)
-        for c in range(QT):
-            nc.scalar.copy(q_bf[:, c, :, :], q_view[:, c, :, :])
+        q_bf = [keep.tile([P, P, PACK], BF16, name=f"q_bf{c}", align_bytes=64) for c in range(QT)]
 
-        dist = keep.tile([P, QT, N], F32, name="dist")
+        def round_queries(c):
+            nc.scalar.copy(
+                q_bf[c][:].rearrange("p (m i) t -> p m t i", i=PACK),
+                q_raw[c][:].rearrange("p t (m i) -> p m t i", i=PACK),
+            )
+
+        round_queries(0)
+
+        round_queries(1)
+        dist = {
+            (0, 0): keep.tile([P, HALF], F32, name="dist00"),
+            (0, 1): late.tile([P, HALF], F32, name="dist01", offset=64, align_bytes=64),
+            (1, 0): late.tile([P, HALF], F32, name="dist10", offset=1088, align_bytes=64),
+            (1, 1): late.tile([P, HALF], F32, name="dist11", offset=2112, align_bytes=64),
+        }
+        spreads = []
         for h in range(HALVES):
             slots = slice(h * HALF, (h + 1) * HALF)
             listed = offsets[:, h * HALF // 16 : (h + 1) * HALF // 16]
             ps_row = keep.tile([P, HALF], F32, name=f"ps_row{h}", align_bytes=64)
             nc.vector.tensor_copy(ps_row[:], ps_pool[:].indirect(listed))
-            turned = psum.tile([P, BLOCKS, P], F32, name=f"turned{h}")
+            turned = psum.tile([P, BLOCKS, P], F32, name=f"turned{h}", tag=f"turned{h}")
             for b in range(BLOCKS):
                 nc.tensor.transpose(turned[:, b, :], ps_row[:, b * P : (b + 1) * P], ident[:])
             ps_col = keep.tile([P, BLOCKS], F32, name=f"ps_col{h}")
@@ -92,19 +110,25 @@ def tile_attend_alibi_topk_kernel(tc, qT, k_words, k_scales, ps, sl, pq, offs, o
                 nc.tensor.transpose(
                     spread[:, b * P : (b + 1) * P], ps_col[:, b : b + 1].to_broadcast([P, P]), ident[:]
                 )
-            for c in range(QT):
-                nc.scalar.activation(dist[:, c, slots], spread[:], ACT.Abs, scale=-1.0, bias=pq_col[:, c : c + 1])
+            spreads.append(spread)
+        for c in range(QT):
+            for h in range(HALVES):
+                nc.scalar.activation(dist[c, h][:], spreads[h][:], ACT.Abs, scale=-1.0, bias=pq_col[:, c, 0:1])
 
         key_scales = keep.tile([P, N], U8, name="key_scales", align_bytes=64)
         nc.vector.tensor_copy(key_scales[:], scale_pool[:].bitcast(U8).indirect(offsets[:]))
 
-        q_codes = keep.tile([P, NQ], U32, name="q_codes", align_bytes=64)
-        q_scales = keep.tile([P, NQ], U8, name="q_scales", align_bytes=64)
-        nc.vector.quantize_mx(
-            out=q_codes[:].bitcast(FP8X4),
-            scales=q_scales[:],
-            in_=q_bf[:].rearrange("p c m t -> p (c m t)"),
-        )
+        q_codes = [keep.tile([P, P], U32, name=f"q_codes{c}", align_bytes=64) for c in range(QT)]
+        q_scales = [keep.tile([P, P], U8, name=f"q_scales{c}", align_bytes=64) for c in range(QT)]
+
+        def quantise(c):
+            nc.vector.quantize_mx(
+                out=q_codes[c][:].bitcast(FP8X4),
+                scales=q_scales[c][:],
+                in_=q_bf[c][:].rearrange("p m t -> p (m t)"),
+            )
+
+        quantise(0)
 
         keys = [
             keep.tile([P, HALF], U32, name="keys0", align_bytes=64),
@@ -114,22 +138,32 @@ def tile_attend_alibi_topk_kernel(tc, qT, k_words, k_scales, ps, sl, pq, offs, o
             listed = offsets[:, h * HALF // 16 : (h + 1) * HALF // 16]
             nc.vector.tensor_copy(keys[h][:], word_pool[:].bitcast(U32).indirect(listed))
 
-        out_rows = out[0].rearrange("(p c) n -> p c n", c=QT)
-        for h in range(HALVES):
-            slots = slice(h * HALF, (h + 1) * HALF)
-            for c in range(QT):
-                scores = psum.tile([P, HALF], F32, name=f"scores{h}_{c}")
-                nc.tensor.matmul_mx(
-                    out=scores[:],
-                    lhsT=q_codes[:, c * P : (c + 1) * P].bitcast(FP8X4),
-                    lhsT_scale=q_scales[:, c * P : (c + 1) * P],
-                    rhs=keys[h][:].bitcast(FP8X4),
-                    rhs_scale=key_scales[:, slots],
-                    start=True,
-                    stop=True,
-                )
+        quantise(1)
+
+        out_rows = out[0].rearrange("(c p) n -> p c n", c=QT)
+        last = (QT - 1, HALVES - 1)
+        for c in range(QT):
+            for h in range(HALVES):
+                width = P if c == QT - 1 else HALF
                 result = keep.tile([P, HALF], F32, name=f"result{h}_{c}")
-                nc.vector.scalar_tensor_tensor(
-                    result[:], dist[:, c, slots], neg_sl[:, c : c + 1], scores[:], ALU.mult, ALU.add
-                )
-                nc.sync.dma_start(out_rows[:, c, slots], result[:])
+                for first in range(0, HALF, width):
+                    cols = slice(first, first + width)
+                    slots = slice(h * HALF + first, h * HALF + first + width)
+                    bank = f"turned{h}" if first else f"scores{h}_{c}"
+                    scores = psum.tile([P, width], F32, name=f"scores{h}_{c}_{first}", tag=bank)
+                    nc.tensor.matmul_mx(
+                        out=scores[:],
+                        lhsT=q_codes[c][:].bitcast(FP8X4),
+                        lhsT_scale=q_scales[c][:],
+                        rhs=keys[h][:, cols].bitcast(FP8X4),
+                        rhs_scale=key_scales[:, slots],
+                        start=True,
+                        stop=True,
+                    )
+                    nc.vector.scalar_tensor_tensor(
+                        result[:, cols], dist[c, h][:, cols], neg_sl[:, c : c + 1], scores[:], ALU.mult, ALU.add
+                    )
+                    if (c, h) == last:
+                        nc.sync.dma_start(out_rows[:, c, slots], result[:, cols])
+                if (c, h) != last:
+                    nc.sync.dma_start(out_rows[:, c, h * HALF : (h + 1) * HALF], result[:])

@@ -62,8 +62,8 @@ def tile_attend_alibi_topk_kernel(tc, qT, k_words, k_scales, ps, sl, pq, offs, o
         nc.sync.dma_start(q_raw[0][:], q_rows[:, :, 0:P])
 
         scale_rows = k_scales[0].bitcast(I32)
-        for quad in range(4):
-            nc.sync.dma_start(scale_pool[32 * quad : 32 * quad + 4, :], scale_rows[4 * quad : 4 * quad + 4, :])
+        for r in range(4):
+            nc.sync.dma_start(scale_pool[r:P:32, :], scale_rows[r:16:4, :])
 
         word_pool = late.tile([P, T], I32, name="word_pool", offset=3264, align_bytes=64)
         nc.sync.dma_start(word_pool[:], k_words[0].rearrange("p n t -> p (n t)").bitcast(I32))

@@ -23,6 +23,9 @@ HALVES = 2
 HALF = N // HALVES
 BLOCKS = HALF // P
 PS_ROW = P - 1
+SCALE_ROWS = D // 32
+SCALE_TOP = P - SCALE_ROWS
+ROW_TOP = P - 2 * QT
 
 
 def tile_attend_alibi_topk_kernel(tc, qT, k_words, k_scales, ps, sl, pq, offs, out):
@@ -36,9 +39,21 @@ def tile_attend_alibi_topk_kernel(tc, qT, k_words, k_scales, ps, sl, pq, offs, o
         nc.sync.dma_start(offsets[:], offs)
 
         scale_pool = keep.tile([P, T // 4], I32, name="scale_pool", align_bytes=64)
+        nc.sync.dma_start(scale_pool[SCALE_TOP:P, :], k_scales[0].bitcast(I32))
+        q_raw = keep.tile([P, PACK, NQ], F32, name="q_raw")
+        nc.sync.dma_start(q_raw[:], qT[0].rearrange("(p t) n -> p t n", t=PACK))
+        word_pool = keep.tile([P, T], I32, name="word_pool", align_bytes=64)
+        nc.sync.dma_start(word_pool[:], k_words[0].rearrange("p n t -> p (n t)").bitcast(I32))
+
         ps_pool = keep.tile([P, T], F32, name="ps_pool", align_bytes=64)
-        zeros = late.tile([P, P], F32, name="zeros", offset=3008, align_bytes=64)
-        nc.vector.memset(scale_pool[:], 0)
+        nc.scalar.dma_start(ps_pool[PS_ROW : PS_ROW + 1, :], ps[0:1, :])
+        rows = keep.tile([P, P], F32, name="rows", align_bytes=64)
+        nc.scalar.dma_start(rows[ROW_TOP : ROW_TOP + QT, :], pq[0].rearrange("(c p) o -> c (p o)", c=QT))
+        nc.scalar.dma_start(rows[ROW_TOP + QT : P, :], sl[0].rearrange("(c p) o -> c (p o)", c=QT))
+
+        key_scales = keep.tile([P, N // 4], I32, name="key_scales", align_bytes=64)
+        zeros = keep.tile([P, P], F32, name="zeros", align_bytes=64)
+        nc.vector.memset(scale_pool[0:SCALE_TOP, :], 0)
         nc.vector.memset(zeros[:], 0.0)
         ident = keep.tile([P, P], F32, name="ident")
         nc.gpsimd.affine_select(
@@ -50,55 +65,31 @@ def tile_attend_alibi_topk_kernel(tc, qT, k_words, k_scales, ps, sl, pq, offs, o
             pattern=[[-1, P]],
             channel_multiplier=1,
         )
-        for first, last in ((0, 255), (255, 512), (512, T)):
-            nc.vector.memset(ps_pool[0:PS_ROW, first:last], 0.0)
-        nc.scalar.dma_start(ps_pool[PS_ROW : PS_ROW + 1, :], ps[0:1, :])
+        nc.vector.memset(key_scales[:], 0)
+        nc.vector.memset(rows[0:ROW_TOP, :], 0.0)
+        nc.vector.memset(ps_pool[0:PS_ROW, :], 0.0)
 
-        q_rows = qT[0].rearrange("(p t) n -> p t n", t=PACK)
-        q_raw = [
-            keep.tile([P, PACK, P], F32, name="q_raw0"),
-            late.tile([P, PACK, P], F32, name="q_raw1", offset=1024, align_bytes=64),
-        ]
-        nc.sync.dma_start(q_raw[0][:], q_rows[:, :, 0:P])
-
-        scale_rows = k_scales[0].bitcast(I32)
+        listed_scales = keep.tile([P, N // 4], I32, name="listed_scales", align_bytes=64)
+        nc.vector.tensor_copy(listed_scales[:].bitcast(U8), scale_pool[:].bitcast(U8).indirect(offsets[:]))
         for r in range(4):
-            nc.sync.dma_start(scale_pool[r:P:32, :], scale_rows[r:16:4, :])
-
-        word_pool = late.tile([P, T], I32, name="word_pool", offset=3264, align_bytes=64)
-        nc.sync.dma_start(word_pool[:], k_words[0].rearrange("p n t -> p (n t)").bitcast(I32))
-
-        pq_col = late.tile([P, QT, 8], F32, name="pq_col", offset=3136, align_bytes=64)
-        sl_col = late.tile([P, QT, 8], F32, name="sl_col", offset=3200, align_bytes=64)
-        with nc.allow_non_contiguous_dma(reason="one value a partition for each query tile"):
-            nc.sync.dma_start(pq_col[:, :, 0:1], pq[0].rearrange("(c p) o -> p c o", c=QT))
-            nc.sync.dma_start(q_raw[1][:], q_rows[:, :, P : 2 * P])
-            nc.sync.dma_start(sl_col[:, :, 0:1], sl[0].rearrange("(c p) o -> p c o", c=QT))
-        neg_sl = keep.tile([P, QT], F32, name="neg_sl")
-        nc.scalar.activation(neg_sl[:], sl_col[:, :, 0], ACT.Copy, scale=-1.0)
+            nc.sync.dma_start(key_scales[r:P:32, :], listed_scales[SCALE_TOP + r : P : 4, :])
 
         q_bf = [keep.tile([P, P, PACK], BF16, name=f"q_bf{c}", align_bytes=64) for c in range(QT)]
-
-        def round_queries(c):
+        for c in range(QT):
             nc.scalar.copy(
                 q_bf[c][:].rearrange("p (m i) t -> p m t i", i=PACK),
-                q_raw[c][:].rearrange("p t (m i) -> p m t i", i=PACK),
+                q_raw[:, :, c * P : (c + 1) * P].rearrange("p t (m i) -> p m t i", i=PACK),
             )
 
-        round_queries(0)
+        columns = psum.tile([P, P], F32, name="columns", tag="scores1_1")
+        nc.tensor.transpose(columns[:], rows[:], ident[:])
+        negated = keep.tile([P, 2 * QT], F32, name="negated")
+        nc.scalar.activation(negated[:], columns[:, ROW_TOP:P], ACT.Copy, scale=-1.0)
 
-        round_queries(1)
-        dist = {
-            (0, 0): keep.tile([P, HALF], F32, name="dist00"),
-            (0, 1): late.tile([P, HALF], F32, name="dist01", offset=64, align_bytes=64),
-            (1, 0): late.tile([P, HALF], F32, name="dist10", offset=1088, align_bytes=64),
-            (1, 1): late.tile([P, HALF], F32, name="dist11", offset=2112, align_bytes=64),
-        }
         spreads = []
         for h in range(HALVES):
-            slots = slice(h * HALF, (h + 1) * HALF)
             listed = offsets[:, h * HALF // 16 : (h + 1) * HALF // 16]
-            ps_row = keep.tile([P, HALF], F32, name=f"ps_row{h}", align_bytes=64)
+            ps_row = late.tile([P, HALF], F32, name=f"ps_row{h}", offset=h * 4 * HALF, align_bytes=64)
             nc.vector.tensor_copy(ps_row[:], ps_pool[:].indirect(listed))
             turned = psum.tile([P, BLOCKS, P], F32, name=f"turned{h}", tag=f"turned{h}")
             for b in range(BLOCKS):
@@ -111,59 +102,51 @@ def tile_attend_alibi_topk_kernel(tc, qT, k_words, k_scales, ps, sl, pq, offs, o
                     spread[:, b * P : (b + 1) * P], ps_col[:, b : b + 1].to_broadcast([P, P]), ident[:]
                 )
             spreads.append(spread)
+        dist = {}
+        for h in range(HALVES):
+            for c in range(QT):
+                dist[c, h] = keep.tile([P, HALF], F32, name=f"dist{c}{h}")
+                nc.scalar.activation(dist[c, h][:], spreads[h][:], ACT.Abs, bias=negated[:, c : c + 1])
+
+        q_codes = late.tile([P, NQ], U32, name="q_codes", offset=0, align_bytes=64)
+        q_scales = keep.tile([P, NQ], U8, name="q_scales", align_bytes=64)
         for c in range(QT):
-            for h in range(HALVES):
-                nc.scalar.activation(dist[c, h][:], spreads[h][:], ACT.Abs, scale=-1.0, bias=pq_col[:, c, 0:1])
-
-        key_scales = keep.tile([P, N], U8, name="key_scales", align_bytes=64)
-        nc.vector.tensor_copy(key_scales[:], scale_pool[:].bitcast(U8).indirect(offsets[:]))
-
-        q_codes = [keep.tile([P, P], U32, name=f"q_codes{c}", align_bytes=64) for c in range(QT)]
-        q_scales = [keep.tile([P, P], U8, name=f"q_scales{c}", align_bytes=64) for c in range(QT)]
-
-        def quantise(c):
             nc.vector.quantize_mx(
-                out=q_codes[c][:].bitcast(FP8X4),
-                scales=q_scales[c][:],
+                out=q_codes[:, c * P : (c + 1) * P].bitcast(FP8X4),
+                scales=q_scales[:, c * P : (c + 1) * P],
                 in_=q_bf[c][:].rearrange("p m t -> p (m t)"),
             )
 
-        quantise(0)
-
-        keys = [
-            keep.tile([P, HALF], U32, name="keys0", align_bytes=64),
-            keep.tile([P, HALF], U32, name="keys1", align_bytes=64),
-        ]
+        keys = late.tile([P, N], U32, name="keys", offset=4 * HALF, align_bytes=64)
         for h in range(HALVES):
             listed = offsets[:, h * HALF // 16 : (h + 1) * HALF // 16]
-            nc.vector.tensor_copy(keys[h][:], word_pool[:].bitcast(U32).indirect(listed))
-
-        quantise(1)
+            nc.vector.tensor_copy(keys[:, h * HALF : (h + 1) * HALF], word_pool[:].bitcast(U32).indirect(listed))
 
         out_rows = out[0].rearrange("(c p) n -> p c n", c=QT)
         last = (QT - 1, HALVES - 1)
-        for c in range(QT):
-            for h in range(HALVES):
-                width = P if c == QT - 1 else HALF
+        for h in range(HALVES):
+            for c in range(QT):
+                slots = slice(h * HALF, (h + 1) * HALF)
+                scores = psum.tile([P, HALF], F32, name=f"scores{h}_{c}", tag=f"scores{h}_{c}")
+                nc.tensor.matmul_mx(
+                    out=scores[:],
+                    lhsT=q_codes[:, c * P : (c + 1) * P].bitcast(FP8X4),
+                    lhsT_scale=q_scales[:, c * P : (c + 1) * P],
+                    rhs=keys[:, slots].bitcast(FP8X4),
+                    rhs_scale=key_scales[:].bitcast(U8)[:, slots],
+                    start=True,
+                    stop=True,
+                )
                 result = keep.tile([P, HALF], F32, name=f"result{h}_{c}")
+                width = P if (c, h) == last else HALF
                 for first in range(0, HALF, width):
                     cols = slice(first, first + width)
-                    slots = slice(h * HALF + first, h * HALF + first + width)
-                    bank = f"turned{h}" if first else f"scores{h}_{c}"
-                    scores = psum.tile([P, width], F32, name=f"scores{h}_{c}_{first}", tag=bank)
-                    nc.tensor.matmul_mx(
-                        out=scores[:],
-                        lhsT=q_codes[c][:].bitcast(FP8X4),
-                        lhsT_scale=q_scales[c][:],
-                        rhs=keys[h][:, cols].bitcast(FP8X4),
-                        rhs_scale=key_scales[:, slots],
-                        start=True,
-                        stop=True,
-                    )
                     nc.vector.scalar_tensor_tensor(
-                        result[:, cols], dist[c, h][:, cols], neg_sl[:, c : c + 1], scores[:], ALU.mult, ALU.add
+                        result[:, cols],
+                        dist[c, h][:, cols],
+                        negated[:, QT + c : QT + c + 1],
+                        scores[:, cols],
+                        ALU.mult,
+                        ALU.add,
                     )
-                    if (c, h) == last:
-                        nc.sync.dma_start(out_rows[:, c, slots], result[:, cols])
-                if (c, h) != last:
-                    nc.sync.dma_start(out_rows[:, c, h * HALF : (h + 1) * HALF], result[:])
+                    nc.sync.dma_start(out_rows[:, c, h * HALF + first : h * HALF + first + width], result[:, cols])

@@ -32,7 +32,6 @@ def tile_attend_alibi_topk_kernel(tc, qT, k_words, k_scales, ps, sl, pq, offs, o
     nc = tc.nc
     with ExitStack() as ctx:
         keep = ctx.enter_context(tc.tile_pool(name="keep", bufs=1))
-        late = ctx.enter_context(tc.tile_pool(name="late", bufs=1))
         psum = ctx.enter_context(tc.psum_pool(name="psum", bufs=1))
 
         offsets = keep.tile([P, N // 16], U16, name="offsets")
@@ -40,6 +39,9 @@ def tile_attend_alibi_topk_kernel(tc, qT, k_words, k_scales, ps, sl, pq, offs, o
 
         scale_pool = keep.tile([P, T // 4], I32, name="scale_pool", align_bytes=64)
         nc.sync.dma_start(scale_pool[SCALE_TOP:P, :], k_scales[0].bitcast(I32))
+        rows = keep.tile([P, P], F32, name="rows", align_bytes=64)
+        nc.sync.dma_start(rows[ROW_TOP : ROW_TOP + QT, :], pq[0].rearrange("(c p) o -> c (p o)", c=QT))
+        nc.sync.dma_start(rows[ROW_TOP + QT : P, :], sl[0].rearrange("(c p) o -> c (p o)", c=QT))
         q_raw = keep.tile([P, PACK, NQ], F32, name="q_raw")
         nc.sync.dma_start(q_raw[:], qT[0].rearrange("(p t) n -> p t n", t=PACK))
         word_pool = keep.tile([P, T], I32, name="word_pool", align_bytes=64)
@@ -47,13 +49,13 @@ def tile_attend_alibi_topk_kernel(tc, qT, k_words, k_scales, ps, sl, pq, offs, o
 
         ps_pool = keep.tile([P, T], F32, name="ps_pool", align_bytes=64)
         nc.scalar.dma_start(ps_pool[PS_ROW : PS_ROW + 1, :], ps[0:1, :])
-        rows = keep.tile([P, P], F32, name="rows", align_bytes=64)
-        nc.scalar.dma_start(rows[ROW_TOP : ROW_TOP + QT, :], pq[0].rearrange("(c p) o -> c (p o)", c=QT))
-        nc.scalar.dma_start(rows[ROW_TOP + QT : P, :], sl[0].rearrange("(c p) o -> c (p o)", c=QT))
 
         key_scales = keep.tile([P, N // 4], I32, name="key_scales", align_bytes=64)
         zeros = keep.tile([P, P], F32, name="zeros", align_bytes=64)
         nc.vector.memset(scale_pool[0:SCALE_TOP, :], 0)
+        nc.vector.memset(key_scales[:], 0)
+        nc.vector.memset(rows[0:ROW_TOP, :], 0.0)
+        nc.vector.memset(ps_pool[0:PS_ROW, :], 0.0)
         nc.vector.memset(zeros[:], 0.0)
         ident = keep.tile([P, P], F32, name="ident")
         nc.gpsimd.affine_select(
@@ -65,14 +67,6 @@ def tile_attend_alibi_topk_kernel(tc, qT, k_words, k_scales, ps, sl, pq, offs, o
             pattern=[[-1, P]],
             channel_multiplier=1,
         )
-        nc.vector.memset(key_scales[:], 0)
-        nc.vector.memset(rows[0:ROW_TOP, :], 0.0)
-        nc.vector.memset(ps_pool[0:PS_ROW, :], 0.0)
-
-        listed_scales = keep.tile([P, N // 4], I32, name="listed_scales", align_bytes=64)
-        nc.vector.tensor_copy(listed_scales[:].bitcast(U8), scale_pool[:].bitcast(U8).indirect(offsets[:]))
-        for r in range(4):
-            nc.sync.dma_start(key_scales[r:P:32, :], listed_scales[SCALE_TOP + r : P : 4, :])
 
         q_bf = [keep.tile([P, P, PACK], BF16, name=f"q_bf{c}", align_bytes=64) for c in range(QT)]
         for c in range(QT):
@@ -86,11 +80,22 @@ def tile_attend_alibi_topk_kernel(tc, qT, k_words, k_scales, ps, sl, pq, offs, o
         negated = keep.tile([P, 2 * QT], F32, name="negated")
         nc.scalar.activation(negated[:], columns[:, ROW_TOP:P], ACT.Copy, scale=-1.0)
 
+        ps_rows = [keep.tile([P, HALF], F32, name=f"ps_row{h}", align_bytes=64) for h in range(HALVES)]
+
+        def gather_positions(h):
+            listed = offsets[:, h * HALF // 16 : (h + 1) * HALF // 16]
+            nc.vector.tensor_copy(ps_rows[h][:], ps_pool[:].indirect(listed))
+
+        gather_positions(0)
+        listed_scales = keep.tile([P, N // 4], I32, name="listed_scales", align_bytes=64)
+        nc.vector.tensor_copy(listed_scales[:].bitcast(U8), scale_pool[:].bitcast(U8).indirect(offsets[:]))
+        for r in range(4):
+            nc.sync.dma_start(key_scales[r:P:32, :], listed_scales[SCALE_TOP + r : P : 4, :])
+        gather_positions(1)
+
         spreads = []
         for h in range(HALVES):
-            listed = offsets[:, h * HALF // 16 : (h + 1) * HALF // 16]
-            ps_row = late.tile([P, HALF], F32, name=f"ps_row{h}", offset=h * 4 * HALF, align_bytes=64)
-            nc.vector.tensor_copy(ps_row[:], ps_pool[:].indirect(listed))
+            ps_row = ps_rows[h]
             turned = psum.tile([P, BLOCKS, P], F32, name=f"turned{h}", tag=f"turned{h}")
             for b in range(BLOCKS):
                 nc.tensor.transpose(turned[:, b, :], ps_row[:, b * P : (b + 1) * P], ident[:])
@@ -108,7 +113,7 @@ def tile_attend_alibi_topk_kernel(tc, qT, k_words, k_scales, ps, sl, pq, offs, o
                 dist[c, h] = keep.tile([P, HALF], F32, name=f"dist{c}{h}")
                 nc.scalar.activation(dist[c, h][:], spreads[h][:], ACT.Abs, bias=negated[:, c : c + 1])
 
-        q_codes = late.tile([P, NQ], U32, name="q_codes", offset=0, align_bytes=64)
+        q_codes = keep.tile([P, NQ], U32, name="q_codes", align_bytes=64)
         q_scales = keep.tile([P, NQ], U8, name="q_scales", align_bytes=64)
         for c in range(QT):
             nc.vector.quantize_mx(
@@ -117,7 +122,7 @@ def tile_attend_alibi_topk_kernel(tc, qT, k_words, k_scales, ps, sl, pq, offs, o
                 in_=q_bf[c][:].rearrange("p m t -> p (m t)"),
             )
 
-        keys = late.tile([P, N], U32, name="keys", offset=4 * HALF, align_bytes=64)
+        keys = keep.tile([P, N], U32, name="keys", align_bytes=64)
         for h in range(HALVES):
             listed = offsets[:, h * HALF // 16 : (h + 1) * HALF // 16]
             nc.vector.tensor_copy(keys[:, h * HALF : (h + 1) * HALF], word_pool[:].bitcast(U32).indirect(listed))

@@ -38,12 +38,12 @@ def tile_attend_alibi_topk_kernel(tc, qT, k_words, k_scales, ps, sl, pq, offs, o
         nc.sync.dma_start(offsets[:], offs)
 
         scale_pool = keep.tile([P, T // 4], I32, name="scale_pool", align_bytes=64)
-        nc.sync.dma_start(scale_pool[SCALE_TOP:P, :], k_scales[0].bitcast(I32))
+        nc.scalar.dma_start(scale_pool[SCALE_TOP:P, :], k_scales[0].bitcast(I32))
+        q_raw = keep.tile([P, PACK, NQ], F32, name="q_raw")
+        nc.sync.dma_start(q_raw[:], qT[0].rearrange("(p t) n -> p t n", t=PACK))
         rows = keep.tile([P, P], F32, name="rows", align_bytes=64)
         nc.sync.dma_start(rows[ROW_TOP : ROW_TOP + QT, :], pq[0].rearrange("(c p) o -> c (p o)", c=QT))
         nc.sync.dma_start(rows[ROW_TOP + QT : P, :], sl[0].rearrange("(c p) o -> c (p o)", c=QT))
-        q_raw = keep.tile([P, PACK, NQ], F32, name="q_raw")
-        nc.sync.dma_start(q_raw[:], qT[0].rearrange("(p t) n -> p t n", t=PACK))
         word_pool = keep.tile([P, T], I32, name="word_pool", align_bytes=64)
         nc.sync.dma_start(word_pool[:], k_words[0].rearrange("p n t -> p (n t)").bitcast(I32))
 
@@ -86,11 +86,11 @@ def tile_attend_alibi_topk_kernel(tc, qT, k_words, k_scales, ps, sl, pq, offs, o
             listed = offsets[:, h * HALF // 16 : (h + 1) * HALF // 16]
             nc.vector.tensor_copy(ps_rows[h][:], ps_pool[:].indirect(listed))
 
-        gather_positions(0)
         listed_scales = keep.tile([P, N // 4], I32, name="listed_scales", align_bytes=64)
         nc.vector.tensor_copy(listed_scales[:].bitcast(U8), scale_pool[:].bitcast(U8).indirect(offsets[:]))
         for r in range(4):
             nc.sync.dma_start(key_scales[r:P:32, :], listed_scales[SCALE_TOP + r : P : 4, :])
+        gather_positions(0)
         gather_positions(1)
 
         spreads = []

@@ -128,30 +128,30 @@ def tile_attend_alibi_topk_kernel(tc, qT, k_words, k_scales, ps, sl, pq, offs, o
             nc.vector.tensor_copy(keys[:, h * HALF : (h + 1) * HALF], word_pool[:].bitcast(U32).indirect(listed))
 
         out_rows = out[0].rearrange("(c p) n -> p c n", c=QT)
-        last = (QT - 1, HALVES - 1)
         for h in range(HALVES):
             for c in range(QT):
-                slots = slice(h * HALF, (h + 1) * HALF)
-                scores = psum.tile([P, HALF], F32, name=f"scores{h}_{c}", tag=f"scores{h}_{c}")
-                nc.tensor.matmul_mx(
-                    out=scores[:],
-                    lhsT=q_codes[:, c * P : (c + 1) * P].bitcast(FP8X4),
-                    lhsT_scale=q_scales[:, c * P : (c + 1) * P],
-                    rhs=keys[:, slots].bitcast(FP8X4),
-                    rhs_scale=key_scales[:].bitcast(U8)[:, slots],
-                    start=True,
-                    stop=True,
-                )
+                width = P if (c, h) == (0, 0) else HALF
                 result = keep.tile([P, HALF], F32, name=f"result{h}_{c}")
-                width = P if (c, h) == last else HALF
                 for first in range(0, HALF, width):
                     cols = slice(first, first + width)
+                    slots = slice(h * HALF + first, h * HALF + first + width)
+                    bank = "turned0" if first else f"scores{h}_{c}"
+                    scores = psum.tile([P, width], F32, name=f"scores{h}_{c}_{first}", tag=bank)
+                    nc.tensor.matmul_mx(
+                        out=scores[:],
+                        lhsT=q_codes[:, c * P : (c + 1) * P].bitcast(FP8X4),
+                        lhsT_scale=q_scales[:, c * P : (c + 1) * P],
+                        rhs=keys[:, slots].bitcast(FP8X4),
+                        rhs_scale=key_scales[:].bitcast(U8)[:, slots],
+                        start=True,
+                        stop=True,
+                    )
                     nc.vector.scalar_tensor_tensor(
                         result[:, cols],
                         dist[c, h][:, cols],
                         negated[:, QT + c : QT + c + 1],
-                        scores[:, cols],
+                        scores[:],
                         ALU.mult,
                         ALU.add,
                     )
-                    nc.sync.dma_start(out_rows[:, c, h * HALF + first : h * HALF + first + width], result[:, cols])
+                    nc.sync.dma_start(out_rows[:, c, slots], result[:, cols])

@@ -130,12 +130,12 @@ def tile_attend_alibi_topk_kernel(tc, qT, k_words, k_scales, ps, sl, pq, offs, o
         out_rows = out[0].rearrange("(c p) n -> p c n", c=QT)
         for h in range(HALVES):
             for c in range(QT):
-                width = P if (c, h) == (0, 0) else HALF
+                width = P if h == 0 else HALF
                 result = keep.tile([P, HALF], F32, name=f"result{h}_{c}")
                 for first in range(0, HALF, width):
                     cols = slice(first, first + width)
                     slots = slice(h * HALF + first, h * HALF + first + width)
-                    bank = "turned0" if first else f"scores{h}_{c}"
+                    bank = f"turned{c}" if first else f"scores{h}_{c}"
                     scores = psum.tile([P, width], F32, name=f"scores{h}_{c}_{first}", tag=bank)
                     nc.tensor.matmul_mx(
                         out=scores[:],
@@ -154,4 +154,7 @@ def tile_attend_alibi_topk_kernel(tc, qT, k_words, k_scales, ps, sl, pq, offs, o
                         ALU.mult,
                         ALU.add,
                     )
-                    nc.sync.dma_start(out_rows[:, c, slots], result[:, cols])
+                    if (c, h) == (0, 0):
+                        nc.sync.dma_start(out_rows[:, c, slots], result[:, cols])
+                if (c, h) != (0, 0):
+                    nc.sync.dma_start(out_rows[:, c, h * HALF : (h + 1) * HALF], result[:])

@@ -36,9 +36,10 @@ def tile_attend_alibi_topk_kernel(tc, qT, k_words, k_scales, ps, sl, pq, offs, o
 
         offsets = keep.tile([P, N // 16], U16, name="offsets")
         nc.sync.dma_start(offsets[:], offs)
-
         scale_pool = keep.tile([P, T // 4], I32, name="scale_pool", align_bytes=64)
         nc.scalar.dma_start(scale_pool[SCALE_TOP:P, :], k_scales[0].bitcast(I32))
+        ps_pool = keep.tile([P, T], F32, name="ps_pool", align_bytes=64)
+        nc.scalar.dma_start(ps_pool[PS_ROW : PS_ROW + 1, :], ps[0:1, :])
         q_raw = keep.tile([P, PACK, NQ], F32, name="q_raw")
         nc.sync.dma_start(q_raw[:], qT[0].rearrange("(p t) n -> p t n", t=PACK))
         rows = keep.tile([P, P], F32, name="rows", align_bytes=64)
@@ -47,16 +48,13 @@ def tile_attend_alibi_topk_kernel(tc, qT, k_words, k_scales, ps, sl, pq, offs, o
         word_pool = keep.tile([P, T], I32, name="word_pool", align_bytes=64)
         nc.sync.dma_start(word_pool[:], k_words[0].rearrange("p n t -> p (n t)").bitcast(I32))
 
-        ps_pool = keep.tile([P, T], F32, name="ps_pool", align_bytes=64)
-        nc.scalar.dma_start(ps_pool[PS_ROW : PS_ROW + 1, :], ps[0:1, :])
-
         key_scales = keep.tile([P, N // 4], I32, name="key_scales", align_bytes=64)
         zeros = keep.tile([P, P], F32, name="zeros", align_bytes=64)
-        nc.vector.memset(scale_pool[0:SCALE_TOP, :], 0)
-        nc.vector.memset(key_scales[:], 0)
-        nc.vector.memset(rows[0:ROW_TOP, :], 0.0)
-        nc.vector.memset(ps_pool[0:PS_ROW, :], 0.0)
         nc.vector.memset(zeros[:], 0.0)
+        nc.vector.memset(scale_pool[0:SCALE_TOP, :], 0)
+        nc.vector.memset(ps_pool[0:PS_ROW, :], 0.0)
+        nc.scalar.activation(rows[0:ROW_TOP, :], zeros[0:ROW_TOP, :], ACT.Copy)
+        nc.vector.memset(key_scales[:], 0)
         ident = keep.tile([P, P], F32, name="ident")
         nc.gpsimd.affine_select(
             out=ident[:],
@@ -68,51 +66,24 @@ def tile_attend_alibi_topk_kernel(tc, qT, k_words, k_scales, ps, sl, pq, offs, o
             channel_multiplier=1,
         )
 
-        q_bf = [keep.tile([P, P, PACK], BF16, name=f"q_bf{c}", align_bytes=64) for c in range(QT)]
-        for c in range(QT):
-            nc.scalar.copy(
-                q_bf[c][:].rearrange("p (m i) t -> p m t i", i=PACK),
-                q_raw[:, :, c * P : (c + 1) * P].rearrange("p t (m i) -> p m t i", i=PACK),
-            )
-
-        columns = psum.tile([P, P], F32, name="columns", tag="scores1_1")
-        nc.tensor.transpose(columns[:], rows[:], ident[:])
-        negated = keep.tile([P, 2 * QT], F32, name="negated")
-        nc.scalar.activation(negated[:], columns[:, ROW_TOP:P], ACT.Copy, scale=-1.0)
-
-        ps_rows = [keep.tile([P, HALF], F32, name=f"ps_row{h}", align_bytes=64) for h in range(HALVES)]
-
-        def gather_positions(h):
-            listed = offsets[:, h * HALF // 16 : (h + 1) * HALF // 16]
-            nc.vector.tensor_copy(ps_rows[h][:], ps_pool[:].indirect(listed))
+        def listed(first, count):
+            return offsets[:, first // 16 : (first + count) // 16]
 
         listed_scales = keep.tile([P, N // 4], I32, name="listed_scales", align_bytes=64)
         nc.vector.tensor_copy(listed_scales[:].bitcast(U8), scale_pool[:].bitcast(U8).indirect(offsets[:]))
         for r in range(4):
             nc.sync.dma_start(key_scales[r:P:32, :], listed_scales[SCALE_TOP + r : P : 4, :])
-        gather_positions(0)
-        gather_positions(1)
 
-        spreads = []
+        ps_rows = [keep.tile([P, HALF], F32, name=f"ps_row{h}", align_bytes=64) for h in range(HALVES)]
         for h in range(HALVES):
-            ps_row = ps_rows[h]
-            turned = psum.tile([P, BLOCKS, P], F32, name=f"turned{h}", tag=f"turned{h}")
-            for b in range(BLOCKS):
-                nc.tensor.transpose(turned[:, b, :], ps_row[:, b * P : (b + 1) * P], ident[:])
-            ps_col = keep.tile([P, BLOCKS], F32, name=f"ps_col{h}")
-            nc.scalar.copy(ps_col[:], turned[:, :, PS_ROW])
-            spread = psum.tile([P, HALF], F32, name=f"spread{h}")
-            for b in range(BLOCKS):
-                nc.tensor.transpose(
-                    spread[:, b * P : (b + 1) * P], ps_col[:, b : b + 1].to_broadcast([P, P]), ident[:]
-                )
-            spreads.append(spread)
-        dist = {}
-        for h in range(HALVES):
-            for c in range(QT):
-                dist[c, h] = keep.tile([P, HALF], F32, name=f"dist{c}{h}")
-                nc.scalar.activation(dist[c, h][:], spreads[h][:], ACT.Abs, bias=negated[:, c : c + 1])
+            nc.scalar.activation(ps_rows[h][:], ps_pool[:].indirect(listed(h * HALF, HALF)), ACT.Copy)
 
+        q_bf = [keep.tile([P, P, PACK], BF16, name=f"q_bf{c}", align_bytes=64) for c in range(QT)]
+        for c in range(QT):
+            nc.vector.tensor_copy(
+                q_bf[c][:].rearrange("p (m i) t -> p m t i", i=PACK),
+                q_raw[:, :, c * P : (c + 1) * P].rearrange("p t (m i) -> p m t i", i=PACK),
+            )
         q_codes = keep.tile([P, NQ], U32, name="q_codes", align_bytes=64)
         q_scales = keep.tile([P, NQ], U8, name="q_scales", align_bytes=64)
         for c in range(QT):
@@ -122,10 +93,37 @@ def tile_attend_alibi_topk_kernel(tc, qT, k_words, k_scales, ps, sl, pq, offs, o
                 in_=q_bf[c][:].rearrange("p m t -> p (m t)"),
             )
 
+        spreads = []
+        for h in range(HALVES):
+            sources = [ps_rows[h][:, b * P : (b + 1) * P] for b in range(BLOCKS)]
+            if h == 0:
+                sources.append(rows[:])
+            turned = psum.tile([P, len(sources), P], F32, name=f"turned{h}", tag=f"turned{h}")
+            for b, source in enumerate(sources):
+                nc.tensor.transpose(turned[:, b, :], source, ident[:])
+            columns = keep.tile([P, len(sources), 2 * QT], F32, name=f"columns{h}")
+            nc.scalar.activation(columns[:], turned[:, :, ROW_TOP:P], ACT.Copy, scale=-1.0)
+            if h == 0:
+                negated = columns[:, BLOCKS, :]
+            spread = psum.tile([P, HALF], F32, name=f"spread{h}")
+            for b in range(BLOCKS):
+                nc.tensor.transpose(
+                    spread[:, b * P : (b + 1) * P],
+                    columns[:, b, 2 * QT - 1 : 2 * QT].to_broadcast([P, P]),
+                    ident[:],
+                )
+            spreads.append(spread)
+        dist = {}
+        for h in range(HALVES):
+            for c in range(QT):
+                dist[c, h] = keep.tile([P, HALF], F32, name=f"dist{c}{h}")
+                nc.scalar.activation(dist[c, h][:], spreads[h][:], ACT.Abs, bias=negated[:, c : c + 1], scale=-1.0)
+
         keys = keep.tile([P, N], U32, name="keys", align_bytes=64)
         for h in range(HALVES):
-            listed = offsets[:, h * HALF // 16 : (h + 1) * HALF // 16]
-            nc.vector.tensor_copy(keys[:, h * HALF : (h + 1) * HALF], word_pool[:].bitcast(U32).indirect(listed))
+            nc.vector.tensor_copy(
+                keys[:, h * HALF : (h + 1) * HALF], word_pool[:].bitcast(U32).indirect(listed(h * HALF, HALF))
+            )
 
         out_rows = out[0].rearrange("(c p) n -> p c n", c=QT)
         for h in range(HALVES):

@@ -120,9 +120,9 @@ def tile_attend_alibi_topk_kernel(tc, qT, k_words, k_scales, ps, sl, pq, offs, o
                 nc.scalar.activation(dist[c, h][:], spreads[h][:], ACT.Abs, bias=negated[:, c : c + 1], scale=-1.0)
 
         keys = keep.tile([P, N], U32, name="keys", align_bytes=64)
-        for h in range(HALVES):
+        for first, count in ((0, P), (P, P), (HALF, HALF)):
             nc.vector.tensor_copy(
-                keys[:, h * HALF : (h + 1) * HALF], word_pool[:].bitcast(U32).indirect(listed(h * HALF, HALF))
+                keys[:, first : first + count], word_pool[:].bitcast(U32).indirect(listed(first, count))
             )
 
         out_rows = out[0].rearrange("(c p) n -> p c n", c=QT)

@@ -120,39 +120,32 @@ def tile_attend_alibi_topk_kernel(tc, qT, k_words, k_scales, ps, sl, pq, offs, o
                 nc.scalar.activation(dist[c, h][:], spreads[h][:], ACT.Abs, bias=negated[:, c : c + 1], scale=-1.0)
 
         keys = keep.tile([P, N], U32, name="keys", align_bytes=64)
-        for first, count in ((0, P), (P, P), (HALF, HALF)):
-            nc.vector.tensor_copy(
-                keys[:, first : first + count], word_pool[:].bitcast(U32).indirect(listed(first, count))
-            )
+        for first in range(0, N, P):
+            nc.vector.tensor_copy(keys[:, first : first + P], word_pool[:].bitcast(U32).indirect(listed(first, P)))
 
         out_rows = out[0].rearrange("(c p) n -> p c n", c=QT)
-        for h in range(HALVES):
-            for c in range(QT):
-                width = P if h == 0 else HALF
-                result = keep.tile([P, HALF], F32, name=f"result{h}_{c}")
-                for first in range(0, HALF, width):
-                    cols = slice(first, first + width)
-                    slots = slice(h * HALF + first, h * HALF + first + width)
-                    bank = f"turned{c}" if first else f"scores{h}_{c}"
-                    scores = psum.tile([P, width], F32, name=f"scores{h}_{c}_{first}", tag=bank)
-                    nc.tensor.matmul_mx(
-                        out=scores[:],
-                        lhsT=q_codes[:, c * P : (c + 1) * P].bitcast(FP8X4),
-                        lhsT_scale=q_scales[:, c * P : (c + 1) * P],
-                        rhs=keys[:, slots].bitcast(FP8X4),
-                        rhs_scale=key_scales[:].bitcast(U8)[:, slots],
-                        start=True,
-                        stop=True,
-                    )
-                    nc.vector.scalar_tensor_tensor(
-                        result[:, cols],
-                        dist[c, h][:, cols],
-                        negated[:, QT + c : QT + c + 1],
-                        scores[:],
-                        ALU.mult,
-                        ALU.add,
-                    )
-                    if (c, h) == (0, 0):
-                        nc.sync.dma_start(out_rows[:, c, slots], result[:, cols])
-                if (c, h) != (0, 0):
-                    nc.sync.dma_start(out_rows[:, c, h * HALF : (h + 1) * HALF], result[:])
+        pieces = [(0, 0, P), (0, P, P), (1, 0, HALF), (0, HALF, HALF), (1, HALF, HALF)]
+        for number, (c, first, width) in enumerate(pieces):
+            bank = "turned0" if number == len(pieces) - 1 else f"scores{number}"
+            scores = psum.tile([P, width], F32, name=f"scores{number}", tag=bank)
+            for at in range(0, width, P):
+                slots = slice(first + at, first + at + P)
+                nc.tensor.matmul_mx(
+                    out=scores[:, at : at + P],
+                    lhsT=q_codes[:, c * P : (c + 1) * P].bitcast(FP8X4),
+                    lhsT_scale=q_scales[:, c * P : (c + 1) * P],
+                    rhs=keys[:, slots].bitcast(FP8X4),
+                    rhs_scale=key_scales[:].bitcast(U8)[:, slots],
+                    start=True,
+                    stop=True,
+                )
+            result = keep.tile([P, width], F32, name=f"result{number}")
+            nc.vector.scalar_tensor_tensor(
+                result[:],
+                dist[c, first // HALF][:, first % HALF : first % HALF + width],
+                negated[:, QT + c : QT + c + 1],
+                scores[:],
+                ALU.mult,
+                ALU.add,
+            )
+            nc.sync.dma_start(out_rows[:, c, first : first + width], result[:])

@@ -25,7 +25,7 @@ BLOCKS = HALF // P
 PS_ROW = P - 1
 SCALE_ROWS = D // 32
 SCALE_TOP = P - SCALE_ROWS
-ROW_TOP = P - 2 * QT
+ROW_TOP = P - QT
 
 
 def tile_attend_alibi_topk_kernel(tc, qT, k_words, k_scales, ps, sl, pq, offs, out):
@@ -43,10 +43,11 @@ def tile_attend_alibi_topk_kernel(tc, qT, k_words, k_scales, ps, sl, pq, offs, o
         q_raw = keep.tile([P, PACK, NQ], F32, name="q_raw")
         nc.sync.dma_start(q_raw[:], qT[0].rearrange("(p t) n -> p t n", t=PACK))
         rows = keep.tile([P, P], F32, name="rows", align_bytes=64)
-        nc.sync.dma_start(rows[ROW_TOP : ROW_TOP + QT, :], pq[0].rearrange("(c p) o -> c (p o)", c=QT))
-        nc.sync.dma_start(rows[ROW_TOP + QT : P, :], sl[0].rearrange("(c p) o -> c (p o)", c=QT))
+        nc.sync.dma_start(rows[ROW_TOP:P, :], pq[0].rearrange("(c p) o -> c (p o)", c=QT))
         word_pool = keep.tile([P, T], I32, name="word_pool", align_bytes=64)
         nc.sync.dma_start(word_pool[:], k_words[0].rearrange("p n t -> p (n t)").bitcast(I32))
+        sl_rows = keep.tile([P, P], F32, name="sl_rows", align_bytes=64)
+        nc.sync.dma_start(sl_rows[ROW_TOP:P, :], sl[0].rearrange("(c p) o -> c (p o)", c=QT))
 
         key_scales = keep.tile([P, N // 4], I32, name="key_scales", align_bytes=64)
         zeros = keep.tile([P, P], F32, name="zeros", align_bytes=64)
@@ -54,6 +55,7 @@ def tile_attend_alibi_topk_kernel(tc, qT, k_words, k_scales, ps, sl, pq, offs, o
         nc.vector.memset(scale_pool[0:SCALE_TOP, :], 0)
         nc.vector.memset(ps_pool[0:PS_ROW, :], 0.0)
         nc.scalar.activation(rows[0:ROW_TOP, :], zeros[0:ROW_TOP, :], ACT.Copy)
+        nc.scalar.activation(sl_rows[0:ROW_TOP, :], zeros[0:ROW_TOP, :], ACT.Copy)
         nc.vector.memset(key_scales[:], 0)
         ident = keep.tile([P, P], F32, name="ident")
         nc.gpsimd.affine_select(
@@ -75,13 +77,13 @@ def tile_attend_alibi_topk_kernel(tc, qT, k_words, k_scales, ps, sl, pq, offs, o
             nc.sync.dma_start(key_scales[r:P:32, :], listed_scales[SCALE_TOP + r : P : 4, :])
 
         ps_rows = [keep.tile([P, HALF], F32, name=f"ps_row{h}", align_bytes=64) for h in range(HALVES)]
-        for h in range(HALVES):
-            nc.scalar.activation(ps_rows[h][:], ps_pool[:].indirect(listed(h * HALF, HALF)), ACT.Copy)
+        nc.scalar.activation(ps_rows[0][:], ps_pool[:].indirect(listed(0, HALF)), ACT.Copy)
+        nc.vector.tensor_copy(ps_rows[1][:], ps_pool[:].indirect(listed(HALF, HALF)))
 
-        q_bf = [keep.tile([P, P, PACK], BF16, name=f"q_bf{c}", align_bytes=64) for c in range(QT)]
+        q_bf = keep.tile([P, NQ, PACK], BF16, name="q_bf", tag="ps_pool", align_bytes=64)
         for c in range(QT):
             nc.vector.tensor_copy(
-                q_bf[c][:].rearrange("p (m i) t -> p m t i", i=PACK),
+                q_bf[:, c * P : (c + 1) * P, :].rearrange("p (m i) t -> p m t i", i=PACK),
                 q_raw[:, :, c * P : (c + 1) * P].rearrange("p t (m i) -> p m t i", i=PACK),
             )
         q_codes = keep.tile([P, NQ], U32, name="q_codes", align_bytes=64)
@@ -90,7 +92,7 @@ def tile_attend_alibi_topk_kernel(tc, qT, k_words, k_scales, ps, sl, pq, offs, o
             nc.vector.quantize_mx(
                 out=q_codes[:, c * P : (c + 1) * P].bitcast(FP8X4),
                 scales=q_scales[:, c * P : (c + 1) * P],
-                in_=q_bf[c][:].rearrange("p m t -> p (m t)"),
+                in_=q_bf[:, c * P : (c + 1) * P, :].rearrange("p m t -> p (m t)"),
             )
 
         spreads = []
@@ -101,7 +103,7 @@ def tile_attend_alibi_topk_kernel(tc, qT, k_words, k_scales, ps, sl, pq, offs, o
             turned = psum.tile([P, len(sources), P], F32, name=f"turned{h}", tag=f"turned{h}")
             for b, source in enumerate(sources):
                 nc.tensor.transpose(turned[:, b, :], source, ident[:])
-            columns = keep.tile([P, len(sources), 2 * QT], F32, name=f"columns{h}")
+            columns = keep.tile([P, len(sources), QT], F32, name=f"columns{h}")
             nc.scalar.activation(columns[:], turned[:, :, ROW_TOP:P], ACT.Copy, scale=-1.0)
             if h == 0:
                 negated = columns[:, BLOCKS, :]
@@ -109,7 +111,7 @@ def tile_attend_alibi_topk_kernel(tc, qT, k_words, k_scales, ps, sl, pq, offs, o
             for b in range(BLOCKS):
                 nc.tensor.transpose(
                     spread[:, b * P : (b + 1) * P],
-                    columns[:, b, 2 * QT - 1 : 2 * QT].to_broadcast([P, P]),
+                    columns[:, b, QT - 1 : QT].to_broadcast([P, P]),
                     ident[:],
                 )
             spreads.append(spread)
@@ -118,6 +120,11 @@ def tile_attend_alibi_topk_kernel(tc, qT, k_words, k_scales, ps, sl, pq, offs, o
             for c in range(QT):
                 dist[c, h] = keep.tile([P, HALF], F32, name=f"dist{c}{h}")
                 nc.scalar.activation(dist[c, h][:], spreads[h][:], ACT.Abs, bias=negated[:, c : c + 1], scale=-1.0)
+
+        sl_turned = psum.tile([P, P], F32, name="sl_turned", tag="turned1")
+        nc.tensor.transpose(sl_turned[:], sl_rows[:], ident[:])
+        sl_negated = keep.tile([P, QT], F32, name="sl_negated")
+        nc.scalar.activation(sl_negated[:], sl_turned[:, ROW_TOP:P], ACT.Copy, scale=-1.0)
 
         keys = keep.tile([P, N], U32, name="keys", align_bytes=64)
         for first in range(0, N, P):
@@ -143,7 +150,7 @@ def tile_attend_alibi_topk_kernel(tc, qT, k_words, k_scales, ps, sl, pq, offs, o
             nc.vector.scalar_tensor_tensor(
                 result[:],
                 dist[c, first // HALF][:, first % HALF : first % HALF + width],
-                negated[:, QT + c : QT + c + 1],
+                sl_negated[:, c : c + 1],
                 scores[:],
                 ALU.mult,
                 ALU.add,

from contextlib import ExitStack

import concourse.mybir as mybir

N, T, D, NQ = 512, 2048, 512, 256
FLOPS = 2 * NQ * N * D
BYTES = 4 * D * NQ + D * T + 16 * T + 4 * T + 8 * NQ + 2 * 128 * (N // 16) + 4 * NQ * N

F32 = mybir.dt.float32
BF16 = mybir.dt.bfloat16
I32 = mybir.dt.int32
U32 = mybir.dt.uint32
U16 = mybir.dt.uint16
U8 = mybir.dt.uint8
FP8X4 = mybir.dt.float8_e4m3fn_x4
ACT = mybir.ActivationFunctionType
ALU = mybir.AluOpType

P = 128
PACK = 4
QT = NQ // P
HALVES = 2
HALF = N // HALVES
BLOCKS = HALF // P
PS_ROW = P - 1
SCALE_ROWS = D // 32
SCALE_TOP = P - SCALE_ROWS
ROW_TOP = P - QT


def tile_attend_alibi_topk_kernel(tc, qT, k_words, k_scales, ps, sl, pq, offs, out):
    nc = tc.nc
    with ExitStack() as ctx:
        keep = ctx.enter_context(tc.tile_pool(name="keep", bufs=1))
        psum = ctx.enter_context(tc.psum_pool(name="psum", bufs=1))

        offsets = keep.tile([P, N // 16], U16, name="offsets")
        nc.sync.dma_start(offsets[:], offs)
        scale_pool = keep.tile([P, T // 4], I32, name="scale_pool", align_bytes=64)
        nc.scalar.dma_start(scale_pool[SCALE_TOP:P, :], k_scales[0].bitcast(I32))
        ps_pool = keep.tile([P, T], F32, name="ps_pool", align_bytes=64)
        nc.scalar.dma_start(ps_pool[PS_ROW : PS_ROW + 1, :], ps[0:1, :])
        q_raw = keep.tile([P, PACK, NQ], F32, name="q_raw")
        nc.sync.dma_start(q_raw[:], qT[0].rearrange("(p t) n -> p t n", t=PACK))
        rows = keep.tile([P, P], F32, name="rows", align_bytes=64)
        nc.sync.dma_start(rows[ROW_TOP:P, :], pq[0].rearrange("(c p) o -> c (p o)", c=QT))
        word_pool = keep.tile([P, T], I32, name="word_pool", align_bytes=64)
        nc.sync.dma_start(word_pool[:], k_words[0].rearrange("p n t -> p (n t)").bitcast(I32))
        sl_rows = keep.tile([P, P], F32, name="sl_rows", align_bytes=64)
        nc.sync.dma_start(sl_rows[ROW_TOP:P, :], sl[0].rearrange("(c p) o -> c (p o)", c=QT))

        key_scales = keep.tile([P, N // 4], I32, name="key_scales", align_bytes=64)
        zeros = keep.tile([P, P], F32, name="zeros", align_bytes=64)
        nc.vector.memset(zeros[:], 0.0)
        nc.vector.memset(scale_pool[0:SCALE_TOP, :], 0)
        nc.vector.memset(ps_pool[0:PS_ROW, :], 0.0)
        nc.scalar.activation(rows[0:ROW_TOP, :], zeros[0:ROW_TOP, :], ACT.Copy)
        nc.scalar.activation(sl_rows[0:ROW_TOP, :], zeros[0:ROW_TOP, :], ACT.Copy)
        nc.vector.memset(key_scales[:], 0)
        ident = keep.tile([P, P], F32, name="ident")
        nc.gpsimd.affine_select(
            out=ident[:],
            in_=zeros[:],
            compare_op=ALU.not_equal,
            fill=1.0,
            base=0,
            pattern=[[-1, P]],
            channel_multiplier=1,
        )

        def listed(first, count):
            return offsets[:, first // 16 : (first + count) // 16]

        listed_scales = keep.tile([P, N // 4], I32, name="listed_scales", align_bytes=64)
        nc.vector.tensor_copy(listed_scales[:].bitcast(U8), scale_pool[:].bitcast(U8).indirect(offsets[:]))
        for r in range(4):
            nc.sync.dma_start(key_scales[r:P:32, :], listed_scales[SCALE_TOP + r : P : 4, :])

        ps_rows = [keep.tile([P, HALF], F32, name=f"ps_row{h}", align_bytes=64) for h in range(HALVES)]
        nc.scalar.activation(ps_rows[0][:], ps_pool[:].indirect(listed(0, HALF)), ACT.Copy)
        nc.vector.tensor_copy(ps_rows[1][:], ps_pool[:].indirect(listed(HALF, HALF)))

        q_bf = keep.tile([P, NQ, PACK], BF16, name="q_bf", tag="ps_pool", align_bytes=64)
        for c in range(QT):
            nc.vector.tensor_copy(
                q_bf[:, c * P : (c + 1) * P, :].rearrange("p (m i) t -> p m t i", i=PACK),
                q_raw[:, :, c * P : (c + 1) * P].rearrange("p t (m i) -> p m t i", i=PACK),
            )
        q_codes = keep.tile([P, NQ], U32, name="q_codes", align_bytes=64)
        q_scales = keep.tile([P, NQ], U8, name="q_scales", align_bytes=64)
        for c in range(QT):
            nc.vector.quantize_mx(
                out=q_codes[:, c * P : (c + 1) * P].bitcast(FP8X4),
                scales=q_scales[:, c * P : (c + 1) * P],
                in_=q_bf[:, c * P : (c + 1) * P, :].rearrange("p m t -> p (m t)"),
            )

        spreads = []
        for h in range(HALVES):
            sources = [ps_rows[h][:, b * P : (b + 1) * P] for b in range(BLOCKS)]
            if h == 0:
                sources.append(rows[:])
            turned = psum.tile([P, len(sources), P], F32, name=f"turned{h}", tag=f"turned{h}")
            for b, source in enumerate(sources):
                nc.tensor.transpose(turned[:, b, :], source, ident[:])
            columns = keep.tile([P, len(sources), QT], F32, name=f"columns{h}")
            nc.scalar.activation(columns[:], turned[:, :, ROW_TOP:P], ACT.Copy, scale=-1.0)
            if h == 0:
                negated = columns[:, BLOCKS, :]
            spread = psum.tile([P, HALF], F32, name=f"spread{h}")
            for b in range(BLOCKS):
                nc.tensor.transpose(
                    spread[:, b * P : (b + 1) * P],
                    columns[:, b, QT - 1 : QT].to_broadcast([P, P]),
                    ident[:],
                )
            spreads.append(spread)
        dist = {}
        for h in range(HALVES):
            for c in range(QT):
                dist[c, h] = keep.tile([P, HALF], F32, name=f"dist{c}{h}")
                nc.scalar.activation(dist[c, h][:], spreads[h][:], ACT.Abs, bias=negated[:, c : c + 1], scale=-1.0)

        sl_turned = psum.tile([P, P], F32, name="sl_turned", tag="turned1")
        nc.tensor.transpose(sl_turned[:], sl_rows[:], ident[:])
        sl_negated = keep.tile([P, QT], F32, name="sl_negated")
        nc.scalar.activation(sl_negated[:], sl_turned[:, ROW_TOP:P], ACT.Copy, scale=-1.0)

        keys = keep.tile([P, N], U32, name="keys", align_bytes=64)
        for first in range(0, N, P):
            nc.vector.tensor_copy(keys[:, first : first + P], word_pool[:].bitcast(U32).indirect(listed(first, P)))

        out_rows = out[0].rearrange("(c p) n -> p c n", c=QT)
        pieces = [(0, 0, P), (0, P, P), (1, 0, HALF), (0, HALF, HALF), (1, HALF, HALF)]
        for number, (c, first, width) in enumerate(pieces):
            bank = "turned0" if number == len(pieces) - 1 else f"scores{number}"
            scores = psum.tile([P, width], F32, name=f"scores{number}", tag=bank)
            for at in range(0, width, P):
                slots = slice(first + at, first + at + P)
                nc.tensor.matmul_mx(
                    out=scores[:, at : at + P],
                    lhsT=q_codes[:, c * P : (c + 1) * P].bitcast(FP8X4),
                    lhsT_scale=q_scales[:, c * P : (c + 1) * P],
                    rhs=keys[:, slots].bitcast(FP8X4),
                    rhs_scale=key_scales[:].bitcast(U8)[:, slots],
                    start=True,
                    stop=True,
                )
            result = keep.tile([P, width], F32, name=f"result{number}")
            nc.vector.scalar_tensor_tensor(
                result[:],
                dist[c, first // HALF][:, first % HALF : first % HALF + width],
                sl_negated[:, c : c + 1],
                scores[:],
                ALU.mult,
                ALU.add,
            )
            nc.sync.dma_start(out_rows[:, c, first : first + width], result[:])
